import numpy as np, ml_dtypes
CORES = [9,25,41,57]
N = 4
BF = ml_dtypes.bfloat16
B, LE, LP, M, ST, RO, TH = 2112, 176, 80, 160, 2, 2, 65536
E = RO * LE + LP
W = B + RO * ST * M
def parts(rng):
    c = (65536 * rng.random((N, 8, 16, B)) * np.exp2(-1.0 * rng.integers(0, 7, (N, 8, 1, B)))).astype(np.int64)
    return c, rng.integers(0, B, (N, 8, 16, B))
def starts(rng, c, share):
    e = np.where(rng.random((N, 8, 1, E)) < share, rng.integers(0, 3, (N, 8, 1, E)), rng.integers(4, 9, (N, 8, 1, E)))
    c[..., B - E:] = (65536 * rng.random((N, 8, 16, E)) * np.exp2(-1.0 * e)).astype(np.int64)
    return c
def pack(c, s):
    return {"c0": np.ascontiguousarray(c.reshape(N, 128, B)).astype(np.int32), "s0": np.ascontiguousarray(s.reshape(N, 128, B)).astype(np.int32)}
def setup_inputs(rng):
    c, s = parts(rng)
    return pack(starts(rng, c, rng.choice(np.array([0.4, 0.7, 0.9, 1.0]), (N, 8, 1, 1))), s)
def setup_inputs_room(rng):
    c, s = parts(rng); c = starts(rng, c, 0.8)
    for q in range(N):
        for g in range(8):
            n = int(rng.choice(np.array([0, 1, M - 1, M, M + 1, LE]))); z = int(rng.choice(np.array([0, 1, LP - 1, LP, LP + 1, M])))
            if q == 0: n = (M, M + 1, LE, M - 1, M, 1, 0, M)[g]; z = (LP, LP + 1, M, LP - 1, 0, 1, 0, 1)[g]
            live = min(n, M); z = min(z, live)
            pool = rng.permutation(B - E); ch = pool[:ST * LE].reshape(ST, LE); nil = pool[ST * LE:ST * LE + 64]; ent = B - E + np.arange(LE)
            who = np.sort(rng.permutation(LE)[:n]); drop = np.delete(who[:M], rng.permutation(live)[:z])
            c[q, g][:, ent] = 0; c[q, g][:, ent[who]] = rng.integers(30000, 65536, (16, n))
            c[q, g][:, ch.reshape(-1)] = rng.integers(20000, 65536, (16, ST * LE)); c[q, g][:, nil] = 0
            c[q, g][:, ch[ST - 1][drop]] = 0
            prev = ent
            for st in range(ST):
                own = np.where(rng.random((16, LE)) < 0.4, ch[st][None, :], rng.choice(nil, (16, LE)))
                own[rng.integers(0, 16, LE), np.arange(LE)] = ch[st]
                s[q, g][:, prev] = own; prev = ch[st]
    return pack(c, s)
def setup_inputs_ties(rng):
    c, s = parts(rng); u = TH // 16
    one = (np.arange(16).reshape(1, 1, 16, 1) == rng.integers(0, 16, (N, 8, 1, B))).astype(np.int64)
    full = rng.random((N, 8, 1, B)) < np.array([0.05, 0.1, 0.2, 0.5, 0.05, 0.1, 0.2, 0.5]).reshape(1, 8, 1, 1)
    c = np.where(full, u, u - one); c = np.where(rng.random((N, 8, 1, B)) < 0.1, 0, c)
    big = rng.random((N, 8, 1, B)) < 0.1; big[:, :4] = False; c = np.where(big, 65535, c)
    c[..., B - E:] = np.where(rng.random((N, 8, 1, E)) < 0.7, 65535, u - one[..., B - E:] * rng.integers(0, 2, (N, 8, 1, E)))
    s[:, :4] = rng.integers(0, B - E, (N, 4, 16, B))
    return pack(c, s)
def setup_inputs_alike(rng):
    c, s = parts(rng); c = starts(rng, c, 0.85)
    for q in range(N):
        for g in range(8):
            h = (1, 2, 17, 64, 160, 300, B // 4, B)[(g + q) % 8]
            s[q, g] = rng.permutation(B)[:h][rng.integers(0, h, (16, B))]
    s = np.where(rng.random(s.shape) < 0.1, np.arange(B), s)
    ends = rng.random(s.shape) < 0.05; ends[:, ::2] = False
    s = np.where(ends, rng.choice(np.array([0, B - 1]), s.shape), s); c[:, 1::2, :, 0] = 65535; c[:, 1::2, :, B - 1] = 65535
    return pack(c, s)
def setup_inputs_links(rng):
    c, s = parts(rng); c = c >> 3; c = starts(rng, c, 0.9)
    near = rng.random(s.shape) < 0.5; near[:, ::2] = True
    return pack(c, np.where(near, rng.integers(B - E, B, s.shape), s))
def setup_inputs_spread(rng):
    c, s = parts(rng); lo = rng.choice(np.array([0.0, 6.0, 10.0]), (N, 8, 1, 1))
    c = np.minimum((np.exp2(lo + (16.0 - lo) * rng.random((N, 8, 1, B))) * rng.random((N, 8, 16, B))).astype(np.int64), 65535)
    c[:, :, :, B - E::7] = rng.integers(0, 65536, c[:, :, :, B - E::7].shape)
    v = rng.random((N, 4, 16, B)); s[:, 1::2] = np.minimum((B * v * v).astype(np.int64), B - 1)
    return pack(c, s)
def check_inputs(d):
    bad = []
    for k, hi in (("c0", 65535), ("s0", B - 1)):
        if np.min(d[k]) < 0 or np.max(d[k]) > hi: bad.append("range of " + k)
    return bad
def reference(c0, s0):
    C = np.zeros((N, 8, 16, W), np.int64); S = np.zeros((N, 8, 16, W), np.int64)
    C[..., :B] = c0.reshape(N, 8, 16, B); S[..., :B] = s0.reshape(N, 8, 16, B)
    port = np.zeros((N, 8, 16, LP), np.int64)
    for rnd in range(RO):
        x = np.concatenate([B - E + rnd * LE + np.arange(LE), B - LP + np.arange(LP)])
        c = np.concatenate([C[..., x[:LE]], port], axis=3)
        for st in range(ST):
            b = B + (rnd * ST + st) * M
            sx = S[..., x]
            score = np.stack([np.add.reduce(np.minimum(c, np.take_along_axis(C, sx[:, :, i][:, :, None, :], 3)), axis=2) for i in range(16)], axis=2)
            k = np.argmax(score, axis=2); best = np.max(score, axis=2)
            y = np.take_along_axis(sx, k[:, :, None, :], 2)[:, :, 0]
            for a in range(N):
                for g in range(8):
                    l = np.flatnonzero(best[a, g] >= TH)
                    l = l[np.sort(np.unique(y[a, g, l], return_index=True)[1])][:M]
                    n = b + np.arange(l.size); yy = y[a, g, l]
                    m = np.minimum(c[a, g][:, l], C[a, g][:, yy]); old = S[a, g][:, yy]
                    C[a, g][:, yy] -= m
                    C[a, g][:, n] = m; S[a, g][:, n] = old
                    S[a, g][k[a, g, l], x[l]] = n
            x = b + np.arange(M); c = np.array(C[..., b:b + M])
        port = np.roll(c[..., :LP], 1, axis=0)
    return {"yc": C.reshape(N, 128, W).astype(np.float32), "ys": np.ascontiguousarray(S[..., B - E:]).reshape(N, 128, W - B + E).astype(np.float32)}

@@ -1,0 +1,454 @@
+from concourse.mybir import AluOpType, ActivationFunctionType
+
+B, LE, LP, M = 2112, 176, 80, 160
+W = B + 4 * M
+CO = 256
+LANES = (176, 160, 256, 160)
+XCOL = (1680, B, 1856, B + 2 * M)
+WIDE = (B, B, B, B + 2 * M)
+CHUNKS = ((96, 80), (96, 64), (128, 128), (96, 64))
+SHARE = ((0, 16), (0, 0), (16, 0), (0, 0))
+
+SCRATCH = {}
+PSUM = ("pK0", "pK1", "pC0", "pC1", "pO0", "pO1", "pY", "pW")
+for _names, _w, _t in (
+        ("CI SI", B, "int32"), ("PI PA", 1, "int32"), ("C", CO + W + 256, "float32"), ("S", W + 256, "float32"),
+        ("G MN", 4096, "float32"), ("EQ", 4096, "bfloat16"), ("DEAD ONEB", 256, "bfloat16"), ("land", LP, "float32"),
+        ("PMX0 PMX1 SEG", 136, "float32"), ("BIAS", 136, "bfloat16"), ("OH0 OH1 IDB BBIG WGT", 128, "bfloat16"),
+        ("OS CY SY DD MV REST TQ EA THA THB THR", 256, "float32"), ("PR YR EV SV0 SV1 SV2 SV3", 256, "float16"),
+        ("RS", 512, "float16"), ("BB1", 128, "float16"), ("BSEL", 2048, "float16"), ("RSEL", 2048, "bfloat16"),
+        ("YO YF YD DX D16 F S2 U16 WN WY LFN LFY QD QE QO T16 I16 IDP TR TRX TRM TN TB", 16, "float32"),
+        ("QH QL", 16, "bfloat16"), ("YG LN LY", 16, "uint16"), ("SX0 SX1 SX2 SX3", 256, "uint16"),
+        ("ONEF BH BONES IDN NEG DG SUM", 128, "float32"), ("KEY8", 8, "float32"), ("PF", 1, "float32")):
+    for _n in _names.split():
+        SCRATCH[_n] = ("sbuf", [128, _w], _t)
+for _n in PSUM:
+    SCRATCH[_n] = ("psum", [128, 512], "float32")
+NDMA = 18
+SEMAPHORES = ["qV", "qA", "qP", "qG", "snt", "arr"] + ["d%d" % _i for _i in range(NDMA)]
+
+
+def R(name, lo, hi, step=1, p=128):
+    return (name, lo, hi, step, p)
+
+
+def IND(win, off):
+    return ("@", win, off)
+
+
+def machine(g, T):
+    queue = {"V": g.vector, "A": g.scalar, "P": g.tensor, "G": g, "S": g.sync}
+    count = {"V": 0, "A": 0, "P": 0, "G": 0}
+    known = {"V": {}, "A": {}, "P": {}, "G": {}, "S": {}}
+    clock = {}
+    log = {}
+    ndma = [0]
+
+    def ap(r):
+        if r[0] == "@":
+            return ap(r[1]).indirect(ap(r[2]))
+        name, lo, hi, step, p = r
+        if step == 1:
+            return T[name][0:p, lo:hi]
+        return T[name][0:p, lo:hi:step]
+
+    def spread(items):
+        out = []
+        for r in items:
+            if not isinstance(r, tuple):
+                continue
+            if r[0] == "@":
+                out.append(r[1])
+                out.append(r[2])
+            else:
+                out.append(r)
+        return out
+
+    def needs(q, reads, writes, compute):
+        need = {}
+        for kind, items in (("r", reads), ("w", writes)):
+            for r in items:
+                name, lo, hi = r[0], r[1], r[2]
+                psum = name in PSUM
+                for (l2, h2, k2, ch, val, q2, c2) in log.get(name, []):
+                    same = q2 == q and c2 and compute
+                    over = lo < h2 and l2 < hi
+                    if psum and not same:
+                        hit = True
+                    elif not over or (kind == "r" and k2 == "r"):
+                        hit = False
+                    elif same:
+                        hit = k2 == "w" and q != "P"
+                    else:
+                        hit = True
+                    if hit:
+                        need[ch] = max(need.get(ch, 0), val)
+        return need
+
+    def wait(q, need):
+        todo = {ch: v for ch, v in need.items() if known[q].get(ch, 0) < v}
+        for ch, v in todo.items():
+            if not any(c2 != ch and clock[(c2, v2)].get(ch, 0) >= v for c2, v2 in todo.items()):
+                queue[q].wait_ge(T.sem[ch], v)
+        for ch, v in todo.items():
+            for c2, v2 in clock[(ch, v)].items():
+                if known[q].get(c2, 0) < v2:
+                    known[q][c2] = v2
+
+    def record(q, ch, val, reads, writes, compute):
+        snap = dict(known[q])
+        if compute:
+            for c2, v2 in clock.get((ch, val - 1), {}).items():
+                if snap.get(c2, 0) < v2:
+                    snap[c2] = v2
+        snap[ch] = val
+        clock[(ch, val)] = snap
+        for kind, items in (("r", reads), ("w", writes)):
+            for r in items:
+                name, lo, hi, full = r[0], r[1], r[2], r[3] == 1 and r[4] == 128
+                old = log.get(name, [])
+                if name in PSUM:
+                    old = [a for a in old if a[5] == q]
+                if kind == "w" and full:
+                    old = [a for a in old if not (lo <= a[0] and a[1] <= hi)]
+                log[name] = old + [(lo, hi, kind, ch, val, q, compute)]
+
+    def op(q, call, out, reads):
+        rd = spread(reads)
+        wr = [out]
+        if out[0] == "@":
+            wr = [(out[1][0], out[1][1], out[1][2], 2, 128)]
+            rd.append(out[2])
+        wait(q, needs(q, rd, wr, True))
+        count[q] += 1
+        ch = "q" + q
+        call(queue[q]).then_inc(T.sem[ch], 1)
+        record(q, ch, count[q], rd, wr, True)
+
+    def dma(q, out, in_, reads, writes):
+        wait(q, needs(q, reads, writes, False))
+        ch = "d%d" % ndma[0]
+        ndma[0] += 1
+        queue[q].dma_start(out, in_).then_inc(T.sem[ch], 16)
+        record(q, ch, 16, reads, writes, False)
+
+    m = {"ap": ap, "dma": dma}
+    m["cp"] = lambda out, a: op("V", lambda e: e.tensor_copy(ap(out), ap(a)), out, [a])
+    m["tt"] = lambda out, a, b, o: op("V", lambda e: e.tensor_tensor(ap(out), ap(a), ap(b), o), out, [a, b])
+
+    def ts(out, a, s1, o0, s2=None, o1=None):
+        x1 = ap(s1) if isinstance(s1, tuple) else s1
+        if o1 is None:
+            op("V", lambda e: e.tensor_scalar(ap(out), ap(a), x1, None, o0), out, [a, s1])
+        else:
+            op("V", lambda e: e.tensor_scalar(ap(out), ap(a), x1, s2, o0, o1), out, [a, s1])
+    m["ts"] = ts
+    m["fill"] = lambda out, c: op("V", lambda e: e.memset(ap(out), c), out, [])
+    m["scan"] = lambda out, a, b, i, o0, o1: op(
+        "V", lambda e: e.tensor_tensor_scan(ap(out), ap(a), ap(b), i, o0, o1), out, [a, b])
+    m["iota"] = lambda out, pat, base, cm, small: op(
+        "G", (lambda e: e.iota(ap(out), pat, base, cm, allow_small_or_imprecise_dtypes=True)) if small else
+        (lambda e: e.iota(ap(out), pat, base, cm)), out, [])
+    m["keep"] = lambda out, a, pat, cond, base, cm: op(
+        "G", lambda e: e.affine_select(ap(out), ap(a), pat, cond, 0.0, base, cm), out, [a])
+    m["mm"] = lambda out, l, r, start, stop: op(
+        "P", lambda e: e.matmul(ap(out), ap(l), ap(r), start, stop), out, [l, r])
+
+    def act(out, a, func, scale=1.0):
+        x = ap(scale) if isinstance(scale, tuple) else scale
+        op("A", lambda e: e.activation(ap(out), ap(a), func, scale=x), out, [a, scale])
+    m["act"] = act
+
+    def remote(call, reads, local, n):
+        wait("G", needs("G", reads, [], False))
+        call()
+        record("G", local, n, reads, [], False)
+    m["remote"] = remote
+
+    def landed(name, lo, hi, ch, n):
+        clock[(ch, n)] = {ch: n}
+        log[name] = [(lo, hi, "w", ch, n, "far", False)]
+    m["landed"] = landed
+
+    def finish(n):
+        need = {"q" + q: count[q] for q in count}
+        for i in range(ndma[0]):
+            need["d%d" % i] = 16
+        need["snt"] = n
+        for ch, v in need.items():
+            if known["G"].get(ch, 0) < v:
+                g.wait_ge(T.sem[ch], v)
+    m["finish"] = finish
+    return m
+
+
+def rank_program(g, core, T, topo):
+    rank = T.rank_of(core)
+    if rank is None:
+        return
+    O, AF = AluOpType, ActivationFunctionType
+    m = machine(g, T)
+    cp, tt, ts, fill, scan, mm, act, dma, ap, iota, keep = (
+        m["cp"], m["tt"], m["ts"], m["fill"], m["scan"], m["mm"], m["act"], m["dma"], m["ap"], m["iota"], m["keep"])
+    n = len(T.cores)
+    nxt, prv = T.cores[(rank + 1) % n], T.cores[(rank - 1) % n]
+    sent = len(topo.engines(core, nxt))
+    m["landed"]("land", 0, LP, "arr", len(topo.engines(prv, core)))
+
+    def load(q, to, src, lo, hi):
+        dma(q, T[to][:, lo:hi], T[src][:, lo:hi], [], [R(to, lo, hi)])
+    cut = (0, 528, 1056, 1584, B)
+    load("S", "CI", "c0", cut[0], cut[1])
+    load("A", "CI", "c0", cut[1], cut[2])
+    load("S", "SI", "s0", 1680, B)
+    load("A", "CI", "c0", cut[3], cut[4])
+    load("S", "CI", "c0", cut[2], cut[3])
+    load("A", "SI", "s0", 0, 840)
+    load("S", "SI", "s0", 840, 1680)
+
+    fill(R("ONEF", 0, 128), 1.0)
+    iota(R("PI", 0, 1), [[0, 1]], 0, 1, False)
+    iota(R("T16", 0, 16), [[16, 16]], 0, 0, True)
+    iota(R("I16", 0, 16), [[1, 16]], 0, 0, True)
+    keep(R("BH", 0, 128), R("ONEF", 0, 128), [[-16, 8], [0, 16]], O.is_ge, 0, 1)
+    keep(R("BONES", 0, 128), R("BH", 0, 128), [[16, 8], [0, 16]], O.is_ge, 15, -1)
+    keep(R("IDN", 0, 128), R("ONEF", 0, 128), [[-1, 128]], O.is_equal, 0, 1)
+    iota(R("BIAS", 0, 136), [[0, 8], [-1, 17]], 15, 0, True)
+    iota(R("ONEB", 0, 256), [[0, 256]], 1, 0, True)
+    iota(R("C", CO + B, CO + W), [[0, W - B]], 0, 0, True)
+    iota(R("S", B, W), [[0, W - B]], 0, 0, True)
+    fill(R("SEG", 0, 136), 1.0)
+    fill(R("THA", 0, 256), 0.5)
+    fill(R("THB", 0, 256), 0.0)
+    fill(R("SEG", 0, 136, 17), 0.0)
+    fill(R("THA", 0, 256, 16), 0.0)
+    fill(R("THB", 0, 256, 16), 65536.0)
+    ts(R("PA", 0, 1), R("PI", 0, 1), 15, O.bitwise_and)
+    scan(R("THR", 0, 256), R("THA", 0, 256), R("THB", 0, 256), 0.0, O.mult, O.add)
+    cp(R("PF", 0, 1), R("PA", 0, 1))
+    ts(R("IDP", 0, 16), R("I16", 0, 16), R("PF", 0, 1), O.is_equal, 16.0, O.mult)
+    fill(R("BSEL", 0, 2048), 0.0)
+    ts(R("TR", 0, 16), R("T16", 0, 16), R("PF", 0, 1), O.add)
+    ts(R("KEY8", 0, 8), R("BONES", 0, 128, 16), 16.0, O.mult)
+    cp(R("BB1", 0, 128), R("BONES", 0, 128))
+    for i in range(8):
+        cp(R("BSEL", 16 * i, 16 * i + 129 * 15 + 1, 129), R("BONES", 16 * i, 16 * i + 16))
+    fill(R("BIAS", 16, 136, 17), 1048576.0)
+    act(R("IDB", 0, 128), R("IDN", 0, 128), AF.Copy)
+    act(R("BBIG", 0, 128), R("BONES", 0, 128), AF.Copy, 65536.0)
+    act(R("NEG", 0, 128), R("IDN", 0, 128), AF.Copy, -1.0)
+    for i in range(16):
+        act(R("RSEL", 128 * i, 128 * i + 128), R("BONES", 0, 128), AF.Copy, R("IDP", i, i + 1))
+    tt(R("DG", 0, 128), R("IDN", 0, 128), R("THR", 0, 128), O.mult)
+    scan(R("SUM", 0, 128), R("ONEF", 0, 128), R("DG", 0, 128), 0.0, O.mult, O.add)
+    ts(R("WGT", 0, 128), R("BONES", 0, 128), R("SUM", 127, 128), O.mult, 0.5, O.mult)
+
+    def encode(u):
+        L, x = LANES[u], XCOL[u]
+        ts(R("EA", 0, L), R("S", x, x + L), 2047.5, O.is_gt, -4096.0, O.mult)
+        tt(R("EV", 0, L), R("EA", 0, L), R("S", x, x + L), O.add)
+        ts(R("SV%d" % u, 0, L), R("EV", 0, L), 1.0, O.add)
+
+    def lists(u):
+        cp(R("SX%d" % u, 0, LANES[u]), R("S", XCOL[u], XCOL[u] + LANES[u]))
+
+    for j in (0, 1, 3, 2):
+        cp(R("C", CO + cut[j], CO + cut[j + 1]), R("CI", cut[j], cut[j + 1]))
+        if j == 1:
+            cp(R("S", 1680, B), R("SI", 1680, B))
+            lists(0)
+
+    def new_counts(u):
+        L, base, nt, l0 = LANES[u], B + M * u, LANES[u] // 16, 0
+        for b, nl in enumerate(CHUNKS[u]):
+            tt(R("MV", l0, l0 + nl), R("CY", l0, l0 + nl), R("pC%d" % b, 0, nl), O.min)
+            l0 += nl
+        cp(IND(R("C", CO + base, CO + W + 256), R("LN", 0, nt)), R("MV", 0, L))
+
+    def new_links(u):
+        cp(IND(R("S", B + M * u, W + 256), R("LN", 0, LANES[u] // 16)), R("SY", 0, LANES[u]))
+
+    def changes(u):
+        nt = LANES[u] // 16
+        tt(R("QD", 0, nt), R("LFN", 0, nt), R("LFY", 0, nt), O.subtract)
+        ts(R("QE", 0, nt), R("QD", 0, nt), float(B + M * u + CO), O.add)
+        tt(R("QO", 0, nt), R("QE", 0, nt), R("S2", 0, nt), O.mult)
+        cp(R("QH", 0, nt), R("QO", 0, nt))
+        tt(R("QL", 0, nt), R("QO", 0, nt), R("QH", 0, nt), O.subtract)
+        for i in range(16):
+            mm(R("pW", i, LANES[u], 16), R("RSEL", 128 * i, 128 * i + 128), R("QH", 0, nt), True, False)
+            mm(R("pW", i, LANES[u], 16), R("RSEL", 128 * i, 128 * i + 128), R("QL", 0, nt), False, True)
+
+    def update_links(u):
+        L, x = LANES[u], XCOL[u]
+        tt(R("TQ", 0, L), R("OS", 0, L), R("pW", 0, L), O.mult)
+        tt(R("S", x, x + L), R("S", x, x + L), R("TQ", 0, L), O.add)
+
+    def send():
+        rid, pid = topo.addr(nxt)[:2]
+        src = CO + B + M
+        m["remote"](lambda: g.remote_dma(out_ap=T.land[:], in_ap=T.C[:, src:src + LP], remote_sem=T.sem.arr,
+                                         local_sem=T.sem.snt, pid=pid, routing_id=rid, dma_engine_mask=topo.mask(core, nxt)),
+                    [R("C", src, src + LP)], "snt", sent)
+
+    def store_links(q, lo, hi):
+        dma(q, T.ys[:, lo - 1680:hi - 1680], T.S[:, lo:hi], [R("S", lo, hi)], [])
+
+    def store_counts(q, lo, hi):
+        dma(q, T.yc[:, lo:hi], T.C[:, CO + lo:CO + hi], [R("C", CO + lo, CO + hi)], [])
+
+    for u in range(4):
+        L, x, wide = LANES[u], XCOL[u], WIDE[u]
+        nt = L // 16
+        n0, n1 = CHUNKS[u]
+        h0, h1 = SHARE[u]
+        win = R("C", CO, CO + wide)
+        SX, SV = "SX%d" % u, "SV%d" % u
+
+        def gather(q, lo, hi):
+            if lo < hi and q == "A":
+                act(R("G", 16 * lo, 16 * hi), IND(win, R(SX, lo, hi)), AF.Copy)
+            elif lo < hi:
+                cp(R("G", 16 * lo, 16 * hi), IND(win, R(SX, lo, hi)))
+
+        def own(b, lo, hi, src):
+            mm(R("pC%d" % b, lo, hi), R("IDN", 0, 128), src, True, True)
+
+        gather("A", 0, n0 - h0)
+        gather("A", n0, L - h1)
+        if u == 0:
+            encode(0)
+            cp(R("S", 0, 840), R("SI", 0, 840))
+            cp(R("S", 840, 1680), R("SI", 840, 1680))
+            ts(R("TRX", 0, 16), R("TR", 0, 16), 1.0 - CO, O.add)
+            ts(R("TRM", 0, 16), R("TR", 0, 16), -16.0, O.mult)
+        elif u == 2:
+            new_counts(1)
+            send()
+            new_links(1)
+            changes(1)
+        else:
+            changes(u - 1)
+            new_counts(u - 1)
+        own(0, 0, n0, R("C", CO + x, CO + x + n0))
+        if u == 2:
+            own(1, 0, LE - n0, R("C", CO + x + n0, CO + x + LE))
+            act(R("pC1", LE - n0, n1), R("land", 0, LP), AF.Copy)
+        else:
+            own(1, 0, n1, R("C", CO + x + n0, CO + x + L))
+        gather("V", n0 - h0, n0)
+        if u > 0:
+            update_links(u - 1)
+            if u == 1:
+                lists(2)
+                store_links("S", 1680, 1856)
+            if u == 2:
+                store_links("S", B, B + 2 * M)
+            if u == 3:
+                store_links("S", 1856, B)
+
+        def keys(b, k):
+            nl, l0 = CHUNKS[u][b], b * n0
+            tt(R("MN", 16 * l0 + k * nl, 16 * l0 + (k + 1) * nl), R("G", 16 * l0 + k, 16 * (l0 + nl), 16),
+               R("pC%d" % b, 0, nl), O.min)
+            if k == 0:
+                mm(R("pK%d" % b, 0, 136, 1, nl), R("ONEB", 0, nl, 1, 1), R("BIAS", 0, 136, 1, 1), True, False)
+            mm(R("pK%d" % b, k, 136, 17, nl), R("MN", 16 * l0 + k * nl, 16 * l0 + (k + 1) * nl), R("KEY8", 0, 8),
+               False, k == 15)
+
+        def best(b):
+            nl = CHUNKS[u][b]
+            K, X = "pK%d" % b, "PMX%d" % b
+            scan(R(X, 0, 136, 1, nl), R("SEG", 0, 136, 1, nl), R(K, 0, 136, 1, nl), 0.0, O.mult, O.max)
+            for j in range(8):
+                ts(R("OH%d" % b, 16 * j, 16 * j + 16, 1, nl), R(K, 17 * j, 17 * j + 16, 1, nl),
+                   R(X, 17 * j + 16, 17 * j + 17, 1, nl), O.is_equal)
+            mm(R("pO%d" % b, 0, nl), R("OH%d" % b, 0, 128, 1, nl), R("IDB", 0, nl, 1, nl), True, True)
+
+        def pick(b):
+            nl, l0 = CHUNKS[u][b], b * n0
+            tt(R("PR", l0, l0 + nl), R("pO%d" % b, 0, nl), R(SV, l0, l0 + nl), O.mult)
+            act(R("OS", l0, l0 + nl), R("pO%d" % b, 0, nl), AF.Copy)
+
+        for k in range(16):
+            keys(0, k)
+        gather("V", L - h1, L)
+        if u:
+            encode(u)
+        for k in range(16):
+            keys(1, k)
+            if k == 5:
+                best(0)
+            if k == 12:
+                pick(0)
+        ts(R("TN", 0, 16), R("TR", 0, 16), float(W - B - M * u), O.add)
+        ts(R("TB", 0, 16), R("TRM", 0, 16), -16.0 * (W - B - M * u + 1), O.add)
+        best(1)
+        pick(1)
+        mm(R("pY", 0, L), R("BB1", 0, 128), R("PR", 0, L), True, True)
+        for i in range(16):
+            mm(R("pK0", 256, 256 + nt), R("BSEL", 128 * i, 128 * i + 128), R("PR", i, L, 16), i == 0, i == 15)
+        cp(R("YR", 0, L), R("pY", 0, L))
+        ts(R("DEAD", 0, L), R("YR", 0, L), 0.0, O.is_equal)
+        mm(R("pW", 0, L), R("BBIG", 0, 128), R("DEAD", 0, L), True, False)
+        cp(R("YO", 0, nt), R("pK0", 256, 256 + nt))
+        ts(R("YF", 0, nt), R("YO", 0, nt), 0.0, O.is_lt, 4096.0, O.mult)
+
+        def same(t):
+            o = 256 * t
+            ts(R("EQ", o + 16 * t, o + L), R("YR", 16 * t, L), R("YO", t, t + 1), O.is_equal)
+            mm(R("pW", 16 * t, 16 * t + 16), R("WGT", 0, 128), R("EQ", o + 16 * t, o + 16 * t + 16), False, t == nt - 1)
+            if t < nt - 1:
+                mm(R("pW", 16 * t + 16, L), R("BBIG", 0, 128), R("EQ", o + 16 * t + 16, o + L), False, False)
+        same(0)
+        tt(R("YD", 0, nt), R("YF", 0, nt), R("YO", 0, nt), O.add)
+        same(1)
+        ts(R("YG", 0, nt), R("YD", 0, nt), -1.0, O.add, 0.0, O.max)
+        act(R("CY", 0, L), IND(win, R("YG", 0, nt)), AF.Copy)
+        act(R("SY", 0, L), IND(R("S", 0, wide), R("YG", 0, nt)), AF.Copy)
+        for t in range(2, nt):
+            same(t)
+        tt(R("DX", 0, nt), R("YD", 0, nt), R("TRX", 0, nt), O.subtract)
+        if u % 2:
+            l0 = 0
+            for b, nl in enumerate(CHUNKS[u]):
+                tt(R("DD", l0, l0 + nl), R("CY", l0, l0 + nl), R("pC%d" % b, 0, nl), O.subtract)
+                l0 += nl
+            act(R("REST", 0, L), R("DD", 0, L), AF.Relu)
+        ts(R("D16", 0, nt), R("DX", 0, nt), 16.0, O.mult)
+        tt(R("RS", L, 2 * L), R("pW", 0, L), R("THR", 0, L), O.is_lt)
+        scan(R("RS", 0, L), R("ONEB", 0, L), R("RS", L, 2 * L), 0.0, O.mult, O.add)
+        for i in range(16):
+            mm(R("pK1", 256, 256 + 2 * nt), R("BSEL", 128 * i, 128 * i + 128), R("RS", i, 2 * L, 16), i == 0, i == 15)
+        if u % 2 == 0:
+            ent = min(L, LE)
+            mm(R("pY", 0, L), R("IDN", 0, 128), R("CY", 0, L), True, False)
+            mm(R("pY", 0, ent), R("NEG", 0, 128), R("C", CO + x, CO + x + ent), False, ent == L)
+            if ent < L:
+                mm(R("pY", ent, L), R("NEG", 0, 128), R("land", 0, LP), False, True)
+            act(R("REST", 0, L), R("pY", 0, L), AF.Relu)
+
+        ts(R("F", 0, nt), R("pK1", 256, 256 + nt), 16.0 * M + 0.5, O.is_le, 1.0 / 256, O.mult)
+        tt(R("U16", 0, nt), R("pK1", 256, 256 + nt), R("TB", 0, nt), O.add)
+        tt(R("S2", 0, nt), R("F", 0, nt), R("pK1", 256 + nt, 256 + 2 * nt), O.mult)
+        tt(R("WN", 0, nt), R("U16", 0, nt), R("S2", 0, nt), O.mult)
+        tt(R("WY", 0, nt), R("D16", 0, nt), R("S2", 0, nt), O.mult)
+        tt(R("LFN", 0, nt), R("WN", 0, nt), R("TN", 0, nt), O.add)
+        tt(R("LFY", 0, nt), R("WY", 0, nt), R("TR", 0, nt), O.add)
+        cp(R("LN", 0, nt), R("LFN", 0, nt))
+        cp(R("LY", 0, nt), R("LFY", 0, nt))
+        if u % 2 == 0:
+            new_links(u)
+            lists(u + 1)
+        cp(IND(R("C", 0, CO + wide), R("LY", 0, nt)), R("REST", 0, L))
+
+    store_counts("S", 0, 1296)
+    store_counts("A", 1296, W - M)
+    new_counts(3)
+    store_counts("S", W - M, W)
+    new_links(3)
+    store_links("A", W - M, W)
+    changes(3)
+    update_links(3)
+    store_links("S", B + 2 * M, W - M)
+    m["finish"](sent)

@@ -2,29 +2,30 @@ from concourse.mybir import AluOpType, ActivationFunctionType
 
 B, LE, LP, M = 2112, 176, 80, 160
 W = B + 4 * M
-CO = 256
+E = W + 256
 LANES = (176, 160, 256, 160)
 XCOL = (1680, B, 1856, B + 2 * M)
 WIDE = (B, B, B, B + 2 * M)
-CHUNKS = ((96, 80), (96, 64), (128, 128), (96, 64))
-SHARE = ((0, 16), (0, 0), (16, 0), (0, 0))
+CHUNKS = ((112, 64), (32, 128), (128, 128), (32, 128))
+SHARE = ((0, 0), (0, 24), (24, 12), (0, 16))
+BEST = ((10, 13), (0, 5), (0, 5), (0, 5))
 
 SCRATCH = {}
 PSUM = ("pK0", "pK1", "pC0", "pC1", "pO0", "pO1", "pY", "pW")
 for _names, _w, _t in (
-        ("CI SI", B, "int32"), ("PI PA", 1, "int32"), ("C", CO + W + 256, "float32"), ("S", W + 256, "float32"),
+        ("CI SI", B, "int32"), ("PI PA", 1, "int32"), ("C S", E, "float32"),
         ("G MN", 4096, "float32"), ("EQ", 4096, "bfloat16"), ("DEAD ONEB", 256, "bfloat16"), ("land", LP, "float32"),
         ("PMX0 PMX1 SEG", 136, "float32"), ("BIAS", 136, "bfloat16"), ("OH0 OH1 IDB BBIG WGT", 128, "bfloat16"),
-        ("OS CY SY DD MV REST TQ EA THA THB THR", 256, "float32"), ("PR YR EV SV0 SV1 SV2 SV3", 256, "float16"),
+        ("OS CY SY DD REST TQ EA EA2 THA THB THR SV1 SV3", 256, "float32"), ("PR YR EV EV2 SV0 SV2", 256, "float16"),
         ("RS", 512, "float16"), ("BB1", 128, "float16"), ("BSEL", 2048, "float16"), ("RSEL", 2048, "bfloat16"),
-        ("YO YF YD DX D16 F S2 U16 WN WY LFN LFY QD QE QO T16 I16 IDP TR TRX TRM TN TB", 16, "float32"),
+        ("YO YF YD DX D16 F S2 U16 WN WY LFN LFY QO T16 I16 IDP TR TRX TRM TB", 16, "float32"),
         ("QH QL", 16, "bfloat16"), ("YG LN LY", 16, "uint16"), ("SX0 SX1 SX2 SX3", 256, "uint16"),
         ("ONEF BH BONES IDN NEG DG SUM", 128, "float32"), ("KEY8", 8, "float32"), ("PF", 1, "float32")):
     for _n in _names.split():
         SCRATCH[_n] = ("sbuf", [128, _w], _t)
 for _n in PSUM:
     SCRATCH[_n] = ("psum", [128, 512], "float32")
-NDMA = 18
+NDMA = 12
 SEMAPHORES = ["qV", "qA", "qP", "qG", "snt", "arr"] + ["d%d" % _i for _i in range(NDMA)]
 
 
@@ -154,9 +155,9 @@ def machine(g, T):
     m["mm"] = lambda out, l, r, start, stop: op(
         "P", lambda e: e.matmul(ap(out), ap(l), ap(r), start, stop), out, [l, r])
 
-    def act(out, a, func, scale=1.0):
+    def act(out, a, func, scale=1.0, bias=0.0):
         x = ap(scale) if isinstance(scale, tuple) else scale
-        op("A", lambda e: e.activation(ap(out), ap(a), func, scale=x), out, [a, scale])
+        op("A", lambda e: e.activation(ap(out), ap(a), func, bias=bias, scale=x), out, [a, scale])
     m["act"] = act
 
     def remote(call, reads, local, n):
@@ -197,14 +198,13 @@ def rank_program(g, core, T, topo):
 
     def load(q, to, src, lo, hi):
         dma(q, T[to][:, lo:hi], T[src][:, lo:hi], [], [R(to, lo, hi)])
-    cut = (0, 528, 1056, 1584, B)
-    load("S", "CI", "c0", cut[0], cut[1])
-    load("A", "CI", "c0", cut[1], cut[2])
-    load("S", "SI", "s0", 1680, B)
-    load("A", "CI", "c0", cut[3], cut[4])
-    load("S", "CI", "c0", cut[2], cut[3])
-    load("A", "SI", "s0", 0, 840)
-    load("S", "SI", "s0", 840, 1680)
+    cut = (0, 960, 1728, B)
+    load("S", "SI", "s0", 1680, 1856)
+    load("A", "CI", "c0", cut[0], cut[1])
+    load("S", "CI", "c0", cut[1], cut[2])
+    load("A", "CI", "c0", cut[2], cut[3])
+    load("S", "SI", "s0", 1856, B)
+    load("A", "SI", "s0", 0, 1680)
 
     fill(R("ONEF", 0, 128), 1.0)
     iota(R("PI", 0, 1), [[0, 1]], 0, 1, False)
@@ -215,7 +215,7 @@ def rank_program(g, core, T, topo):
     keep(R("IDN", 0, 128), R("ONEF", 0, 128), [[-1, 128]], O.is_equal, 0, 1)
     iota(R("BIAS", 0, 136), [[0, 8], [-1, 17]], 15, 0, True)
     iota(R("ONEB", 0, 256), [[0, 256]], 1, 0, True)
-    iota(R("C", CO + B, CO + W), [[0, W - B]], 0, 0, True)
+    iota(R("C", B, W), [[0, W - B]], 0, 0, True)
     iota(R("S", B, W), [[0, W - B]], 0, 0, True)
     fill(R("SEG", 0, 136), 1.0)
     fill(R("THA", 0, 256), 0.5)
@@ -226,9 +226,9 @@ def rank_program(g, core, T, topo):
     ts(R("PA", 0, 1), R("PI", 0, 1), 15, O.bitwise_and)
     scan(R("THR", 0, 256), R("THA", 0, 256), R("THB", 0, 256), 0.0, O.mult, O.add)
     cp(R("PF", 0, 1), R("PA", 0, 1))
-    ts(R("IDP", 0, 16), R("I16", 0, 16), R("PF", 0, 1), O.is_equal, 16.0, O.mult)
+    ts(R("IDP", 0, 16), R("I16", 0, 16), R("PF", 0, 1), O.is_equal)
     fill(R("BSEL", 0, 2048), 0.0)
-    ts(R("TR", 0, 16), R("T16", 0, 16), R("PF", 0, 1), O.add)
+    ts(R("TR", 0, 16), R("T16", 0, 16), R("PF", 0, 1), O.add, float(W), O.add)
     ts(R("KEY8", 0, 8), R("BONES", 0, 128, 16), 16.0, O.mult)
     cp(R("BB1", 0, 128), R("BONES", 0, 128))
     for i in range(8):
@@ -243,36 +243,38 @@ def rank_program(g, core, T, topo):
     scan(R("SUM", 0, 128), R("ONEF", 0, 128), R("DG", 0, 128), 0.0, O.mult, O.add)
     ts(R("WGT", 0, 128), R("BONES", 0, 128), R("SUM", 127, 128), O.mult, 0.5, O.mult)
 
-    def encode(u):
-        L, x = LANES[u], XCOL[u]
-        ts(R("EA", 0, L), R("S", x, x + L), 2047.5, O.is_gt, -4096.0, O.mult)
-        tt(R("EV", 0, L), R("EA", 0, L), R("S", x, x + L), O.add)
-        ts(R("SV%d" % u, 0, L), R("EV", 0, L), 1.0, O.add)
+    def high(u, to):
+        ts(R(to, 0, LANES[u]), R("S", XCOL[u], XCOL[u] + LANES[u]), 2047.5, O.is_gt, -4096.0, O.mult)
+
+    def total(u, a, to):
+        tt(R(to, 0, LANES[u]), R(a, 0, LANES[u]), R("S", XCOL[u], XCOL[u] + LANES[u]), O.add)
+
+    def plus_one(u, a):
+        ts(R("SV%d" % u, 0, LANES[u]), R(a, 0, LANES[u]), 1.0, O.add)
 
     def lists(u):
         cp(R("SX%d" % u, 0, LANES[u]), R("S", XCOL[u], XCOL[u] + LANES[u]))
 
-    for j in (0, 1, 3, 2):
-        cp(R("C", CO + cut[j], CO + cut[j + 1]), R("CI", cut[j], cut[j + 1]))
-        if j == 1:
-            cp(R("S", 1680, B), R("SI", 1680, B))
-            lists(0)
+    def convert(to, src, lo, hi):
+        cp(R(to, lo, hi), R(src, lo, hi))
+
+    convert("S", "SI", 1680, 1856)
+    lists(0)
+    high(0, "EA")
+    total(0, "EA", "EV")
+    plus_one(0, "EV")
+    for j in (0, 1, 2):
+        convert("C", "CI", cut[j], cut[j + 1])
 
     def new_counts(u):
-        L, base, nt, l0 = LANES[u], B + M * u, LANES[u] // 16, 0
-        for b, nl in enumerate(CHUNKS[u]):
-            tt(R("MV", l0, l0 + nl), R("CY", l0, l0 + nl), R("pC%d" % b, 0, nl), O.min)
-            l0 += nl
-        cp(IND(R("C", CO + base, CO + W + 256), R("LN", 0, nt)), R("MV", 0, L))
+        tt(IND(R("C", B + M * u, E), R("LN", 0, LANES[u] // 16)), R("CY", 0, LANES[u]), R("REST", 0, LANES[u]), O.subtract)
 
     def new_links(u):
-        cp(IND(R("S", B + M * u, W + 256), R("LN", 0, LANES[u] // 16)), R("SY", 0, LANES[u]))
+        cp(IND(R("S", B + M * u, E), R("LN", 0, LANES[u] // 16)), R("SY", 0, LANES[u]))
 
     def changes(u):
         nt = LANES[u] // 16
-        tt(R("QD", 0, nt), R("LFN", 0, nt), R("LFY", 0, nt), O.subtract)
-        ts(R("QE", 0, nt), R("QD", 0, nt), float(B + M * u + CO), O.add)
-        tt(R("QO", 0, nt), R("QE", 0, nt), R("S2", 0, nt), O.mult)
+        tt(R("QO", 0, nt), R("LFN", 0, nt), R("LFY", 0, nt), O.subtract)
         cp(R("QH", 0, nt), R("QO", 0, nt))
         tt(R("QL", 0, nt), R("QO", 0, nt), R("QH", 0, nt), O.subtract)
         for i in range(16):
@@ -282,11 +284,16 @@ def rank_program(g, core, T, topo):
     def update_links(u):
         L, x = LANES[u], XCOL[u]
         tt(R("TQ", 0, L), R("OS", 0, L), R("pW", 0, L), O.mult)
-        tt(R("S", x, x + L), R("S", x, x + L), R("TQ", 0, L), O.add)
+        if u % 2:
+            tt(R("S", x, x + L), R("S", x, x + L), R("TQ", 0, L), O.add)
+        else:
+            mm(R("pW", 0, L), R("IDN", 0, 128), R("S", x, x + L), True, False)
+            mm(R("pW", 0, L), R("IDN", 0, 128), R("TQ", 0, L), False, True)
+            act(R("S", x, x + L), R("pW", 0, L), AF.Copy)
 
     def send():
         rid, pid = topo.addr(nxt)[:2]
-        src = CO + B + M
+        src = B + M
         m["remote"](lambda: g.remote_dma(out_ap=T.land[:], in_ap=T.C[:, src:src + LP], remote_sem=T.sem.arr,
                                          local_sem=T.sem.snt, pid=pid, routing_id=rid, dma_engine_mask=topo.mask(core, nxt)),
                     [R("C", src, src + LP)], "snt", sent)
@@ -295,14 +302,14 @@ def rank_program(g, core, T, topo):
         dma(q, T.ys[:, lo - 1680:hi - 1680], T.S[:, lo:hi], [R("S", lo, hi)], [])
 
     def store_counts(q, lo, hi):
-        dma(q, T.yc[:, lo:hi], T.C[:, CO + lo:CO + hi], [R("C", CO + lo, CO + hi)], [])
+        dma(q, T.yc[:, lo:hi], T.C[:, lo:hi], [R("C", lo, hi)], [])
 
     for u in range(4):
         L, x, wide = LANES[u], XCOL[u], WIDE[u]
         nt = L // 16
         n0, n1 = CHUNKS[u]
         h0, h1 = SHARE[u]
-        win = R("C", CO, CO + wide)
+        win = R("C", 0, wide)
         SX, SV = "SX%d" % u, "SV%d" % u
 
         def gather(q, lo, hi):
@@ -317,35 +324,31 @@ def rank_program(g, core, T, topo):
         gather("A", 0, n0 - h0)
         gather("A", n0, L - h1)
         if u == 0:
-            encode(0)
-            cp(R("S", 0, 840), R("SI", 0, 840))
-            cp(R("S", 840, 1680), R("SI", 840, 1680))
-            ts(R("TRX", 0, 16), R("TR", 0, 16), 1.0 - CO, O.add)
+            ts(R("TRX", 0, 16), R("TR", 0, 16), 1.0, O.add)
             ts(R("TRM", 0, 16), R("TR", 0, 16), -16.0, O.mult)
-        elif u == 2:
-            new_counts(1)
-            send()
-            new_links(1)
-            changes(1)
+            convert("S", "SI", 1856, B)
+            convert("S", "SI", 0, 1680)
         else:
             changes(u - 1)
+            if u % 2:
+                high(u, "EA")
             new_counts(u - 1)
-        own(0, 0, n0, R("C", CO + x, CO + x + n0))
+            if u == 2:
+                send()
+                new_links(1)
+                update_links(1)
+                store_links("S", B, B + 2 * M)
+        own(0, 0, n0, R("C", x, x + n0))
         if u == 2:
-            own(1, 0, LE - n0, R("C", CO + x + n0, CO + x + LE))
+            own(1, 0, LE - n0, R("C", x + n0, x + LE))
             act(R("pC1", LE - n0, n1), R("land", 0, LP), AF.Copy)
         else:
-            own(1, 0, n1, R("C", CO + x + n0, CO + x + L))
+            own(1, 0, n1, R("C", x + n0, x + L))
+        if u % 2:
+            mm(R("pY", 0, L), R("IDN", 0, 128), R("S", x, x + L), True, False)
+            mm(R("pY", 0, L), R("IDN", 0, 128), R("EA", 0, L), False, True)
+            act(R(SV, 0, L), R("pY", 0, L), AF.Identity, 1.0, 1.0)
         gather("V", n0 - h0, n0)
-        if u > 0:
-            update_links(u - 1)
-            if u == 1:
-                lists(2)
-                store_links("S", 1680, 1856)
-            if u == 2:
-                store_links("S", B, B + 2 * M)
-            if u == 3:
-                store_links("S", 1856, B)
 
         def keys(b, k):
             nl, l0 = CHUNKS[u][b], b * n0
@@ -372,17 +375,18 @@ def rank_program(g, core, T, topo):
 
         for k in range(16):
             keys(0, k)
+        if u % 2:
+            lo, hi = ((1680, 1856), (1856, B))[u // 2]
+            update_links(u - 1)
+            store_links("S", lo, hi)
         gather("V", L - h1, L)
-        if u:
-            encode(u)
         for k in range(16):
-            keys(1, k)
-            if k == 5:
+            if k == BEST[u][0]:
                 best(0)
-            if k == 12:
+            keys(1, k)
+            if k == BEST[u][1]:
                 pick(0)
-        ts(R("TN", 0, 16), R("TR", 0, 16), float(W - B - M * u), O.add)
-        ts(R("TB", 0, 16), R("TRM", 0, 16), -16.0 * (W - B - M * u + 1), O.add)
+        ts(R("TB", 0, 16), R("TRM", 0, 16), 16.0 * (B + M * u - 1), O.add)
         best(1)
         pick(1)
         mm(R("pY", 0, L), R("BB1", 0, 128), R("PR", 0, L), True, True)
@@ -420,35 +424,43 @@ def rank_program(g, core, T, topo):
         scan(R("RS", 0, L), R("ONEB", 0, L), R("RS", L, 2 * L), 0.0, O.mult, O.add)
         for i in range(16):
             mm(R("pK1", 256, 256 + 2 * nt), R("BSEL", 128 * i, 128 * i + 128), R("RS", i, 2 * L, 16), i == 0, i == 15)
+        if u == 0:
+            lists(2)
+            high(2, "EA2")
+        if u == 1:
+            total(2, "EA2", "EV2")
+            plus_one(2, "EV2")
         if u % 2 == 0:
             ent = min(L, LE)
             mm(R("pY", 0, L), R("IDN", 0, 128), R("CY", 0, L), True, False)
-            mm(R("pY", 0, ent), R("NEG", 0, 128), R("C", CO + x, CO + x + ent), False, ent == L)
+            mm(R("pY", 0, ent), R("NEG", 0, 128), R("C", x, x + ent), False, ent == L)
             if ent < L:
                 mm(R("pY", ent, L), R("NEG", 0, 128), R("land", 0, LP), False, True)
             act(R("REST", 0, L), R("pY", 0, L), AF.Relu)
 
-        ts(R("F", 0, nt), R("pK1", 256, 256 + nt), 16.0 * M + 0.5, O.is_le, 1.0 / 256, O.mult)
-        tt(R("U16", 0, nt), R("pK1", 256, 256 + nt), R("TB", 0, nt), O.add)
-        tt(R("S2", 0, nt), R("F", 0, nt), R("pK1", 256 + nt, 256 + 2 * nt), O.mult)
-        tt(R("WN", 0, nt), R("U16", 0, nt), R("S2", 0, nt), O.mult)
+        if L > M:
+            ts(R("F", 0, nt), R("pK1", 256, 256 + nt), 16.0 * M + 0.5, O.is_le, 1.0 / 256, O.mult)
+            tt(R("U16", 0, nt), R("pK1", 256, 256 + nt), R("TB", 0, nt), O.add)
+            tt(R("S2", 0, nt), R("F", 0, nt), R("pK1", 256 + nt, 256 + 2 * nt), O.mult)
+        else:
+            ts(R("S2", 0, nt), R("pK1", 256 + nt, 256 + 2 * nt), 1.0 / 256, O.mult)
+            tt(R("U16", 0, nt), R("pK1", 256, 256 + nt), R("TB", 0, nt), O.add)
         tt(R("WY", 0, nt), R("D16", 0, nt), R("S2", 0, nt), O.mult)
-        tt(R("LFN", 0, nt), R("WN", 0, nt), R("TN", 0, nt), O.add)
+        tt(R("WN", 0, nt), R("U16", 0, nt), R("S2", 0, nt), O.mult)
         tt(R("LFY", 0, nt), R("WY", 0, nt), R("TR", 0, nt), O.add)
-        cp(R("LN", 0, nt), R("LFN", 0, nt))
+        tt(R("LFN", 0, nt), R("WN", 0, nt), R("TR", 0, nt), O.add)
         cp(R("LY", 0, nt), R("LFY", 0, nt))
+        ts(R("LN", 0, nt), R("LFN", 0, nt), -float(B + M * u), O.add)
         if u % 2 == 0:
             new_links(u)
             lists(u + 1)
-        cp(IND(R("C", 0, CO + wide), R("LY", 0, nt)), R("REST", 0, L))
+        cp(IND(R("C", 0, E), R("LY", 0, nt)), R("REST", 0, L))
 
-    store_counts("S", 0, 1296)
-    store_counts("A", 1296, W - M)
-    new_counts(3)
-    store_counts("S", W - M, W)
-    new_links(3)
-    store_links("A", W - M, W)
+    store_counts("S", 0, W - M)
     changes(3)
+    new_counts(3)
+    store_counts("A", W - M, W)
+    new_links(3)
     update_links(3)
-    store_links("S", B + 2 * M, W - M)
+    store_links("S", B + 2 * M, W)
     m["finish"](sent)

@@ -7,8 +7,8 @@ LANES = (176, 160, 256, 160)
 XCOL = (1680, B, 1856, B + 2 * M)
 WIDE = (B, B, B, B + 2 * M)
 CHUNKS = ((112, 64), (32, 128), (128, 128), (32, 128))
-SHARE = ((0, 0), (0, 24), (24, 12), (0, 16))
-BEST = ((10, 13), (0, 5), (0, 5), (0, 5))
+SHARE = ((32, 0), (16, 32), (48, 12), (0, 16))
+BEST = ((11, 13), (0, 15), (0, 5), (0, 5))
 
 SCRATCH = {}
 PSUM = ("pK0", "pK1", "pC0", "pC1", "pO0", "pO1", "pY", "pW")
@@ -16,16 +16,17 @@ for _names, _w, _t in (
         ("CI SI", B, "int32"), ("PI PA", 1, "int32"), ("C S", E, "float32"),
         ("G MN", 4096, "float32"), ("EQ", 4096, "bfloat16"), ("DEAD ONEB", 256, "bfloat16"), ("land", LP, "float32"),
         ("PMX0 PMX1 SEG", 136, "float32"), ("BIAS", 136, "bfloat16"), ("OH0 OH1 IDB BBIG WGT", 128, "bfloat16"),
-        ("OS CY SY DD REST TQ EA EA2 THA THB THR SV1 SV3", 256, "float32"), ("PR YR EV EV2 SV0 SV2", 256, "float16"),
+        ("OS CY SY0 SY1 DD REST TQ EA EA2 THA THB THR SV0 SV1 SV3", 256, "float32"), ("PR YR EV2 SV2", 256, "float16"),
         ("RS", 512, "float16"), ("BB1", 128, "float16"), ("BSEL", 2048, "float16"), ("RSEL", 2048, "bfloat16"),
-        ("YO YF YD DX D16 F S2 U16 WN WY LFN LFY QO T16 I16 IDP TR TRX TRM TB", 16, "float32"),
+        ("YO YF YD DX D16 F S2 U16 WN WY LFN LFY QO I16 IDP TR TRX TRM TB", 16, "float32"),
         ("QH QL", 16, "bfloat16"), ("YG LN LY", 16, "uint16"), ("SX0 SX1 SX2 SX3", 256, "uint16"),
+        ("T16", B // 16, "float32"), ("IDL", B // 16, "uint16"),
         ("ONEF BH BONES IDN NEG DG SUM", 128, "float32"), ("KEY8", 8, "float32"), ("PF", 1, "float32")):
     for _n in _names.split():
         SCRATCH[_n] = ("sbuf", [128, _w], _t)
 for _n in PSUM:
     SCRATCH[_n] = ("psum", [128, 512], "float32")
-NDMA = 12
+NDMA = 13
 SEMAPHORES = ["qV", "qA", "qP", "qG", "snt", "arr"] + ["d%d" % _i for _i in range(NDMA)]
 
 
@@ -198,7 +199,7 @@ def rank_program(g, core, T, topo):
 
     def load(q, to, src, lo, hi):
         dma(q, T[to][:, lo:hi], T[src][:, lo:hi], [], [R(to, lo, hi)])
-    cut = (0, 960, 1728, B)
+    cut = (0, 960, 1680, B)
     load("S", "SI", "s0", 1680, 1856)
     load("A", "CI", "c0", cut[0], cut[1])
     load("S", "CI", "c0", cut[1], cut[2])
@@ -208,7 +209,7 @@ def rank_program(g, core, T, topo):
 
     fill(R("ONEF", 0, 128), 1.0)
     iota(R("PI", 0, 1), [[0, 1]], 0, 1, False)
-    iota(R("T16", 0, 16), [[16, 16]], 0, 0, True)
+    iota(R("T16", 0, B // 16), [[16, B // 16]], 0, 0, True)
     iota(R("I16", 0, 16), [[1, 16]], 0, 0, True)
     keep(R("BH", 0, 128), R("ONEF", 0, 128), [[-16, 8], [0, 16]], O.is_ge, 0, 1)
     keep(R("BONES", 0, 128), R("BH", 0, 128), [[16, 8], [0, 16]], O.is_ge, 15, -1)
@@ -229,6 +230,7 @@ def rank_program(g, core, T, topo):
     ts(R("IDP", 0, 16), R("I16", 0, 16), R("PF", 0, 1), O.is_equal)
     fill(R("BSEL", 0, 2048), 0.0)
     ts(R("TR", 0, 16), R("T16", 0, 16), R("PF", 0, 1), O.add, float(W), O.add)
+    ts(R("IDL", 0, B // 16), R("T16", 0, B // 16), R("PF", 0, 1), O.add)
     ts(R("KEY8", 0, 8), R("BONES", 0, 128, 16), 16.0, O.mult)
     cp(R("BB1", 0, 128), R("BONES", 0, 128))
     for i in range(8):
@@ -246,12 +248,6 @@ def rank_program(g, core, T, topo):
     def high(u, to):
         ts(R(to, 0, LANES[u]), R("S", XCOL[u], XCOL[u] + LANES[u]), 2047.5, O.is_gt, -4096.0, O.mult)
 
-    def total(u, a, to):
-        tt(R(to, 0, LANES[u]), R(a, 0, LANES[u]), R("S", XCOL[u], XCOL[u] + LANES[u]), O.add)
-
-    def plus_one(u, a):
-        ts(R("SV%d" % u, 0, LANES[u]), R(a, 0, LANES[u]), 1.0, O.add)
-
     def lists(u):
         cp(R("SX%d" % u, 0, LANES[u]), R("S", XCOL[u], XCOL[u] + LANES[u]))
 
@@ -261,16 +257,14 @@ def rank_program(g, core, T, topo):
     convert("S", "SI", 1680, 1856)
     lists(0)
     high(0, "EA")
-    total(0, "EA", "EV")
-    plus_one(0, "EV")
-    for j in (0, 1, 2):
-        convert("C", "CI", cut[j], cut[j + 1])
+    convert("C", "CI", cut[0], cut[1])
+    convert("C", "CI", cut[1], cut[2])
 
     def new_counts(u):
         tt(IND(R("C", B + M * u, E), R("LN", 0, LANES[u] // 16)), R("CY", 0, LANES[u]), R("REST", 0, LANES[u]), O.subtract)
 
     def new_links(u):
-        cp(IND(R("S", B + M * u, E), R("LN", 0, LANES[u] // 16)), R("SY", 0, LANES[u]))
+        cp(IND(R("S", B + M * u, E), R("LN", 0, LANES[u] // 16)), R("SY%d" % (u % 2), 0, LANES[u]))
 
     def changes(u):
         nt = LANES[u] // 16
@@ -281,10 +275,12 @@ def rank_program(g, core, T, topo):
             mm(R("pW", i, LANES[u], 16), R("RSEL", 128 * i, 128 * i + 128), R("QH", 0, nt), True, False)
             mm(R("pW", i, LANES[u], 16), R("RSEL", 128 * i, 128 * i + 128), R("QL", 0, nt), False, True)
 
-    def update_links(u):
+    def link_changes(u):
+        tt(R("TQ", 0, LANES[u]), R("OS", 0, LANES[u]), R("pW", 0, LANES[u]), O.mult)
+
+    def add_links(u):
         L, x = LANES[u], XCOL[u]
-        tt(R("TQ", 0, L), R("OS", 0, L), R("pW", 0, L), O.mult)
-        if u % 2:
+        if u == 3:
             tt(R("S", x, x + L), R("S", x, x + L), R("TQ", 0, L), O.add)
         else:
             mm(R("pW", 0, L), R("IDN", 0, 128), R("S", x, x + L), True, False)
@@ -309,8 +305,8 @@ def rank_program(g, core, T, topo):
         nt = L // 16
         n0, n1 = CHUNKS[u]
         h0, h1 = SHARE[u]
-        win = R("C", 0, wide)
-        SX, SV = "SX%d" % u, "SV%d" % u
+        win = R("C" if u else "CI", 0, wide)
+        SX, SV, SY = "SX%d" % u, "SV%d" % u, "SY%d" % (u % 2)
 
         def gather(q, lo, hi):
             if lo < hi and q == "A":
@@ -324,10 +320,7 @@ def rank_program(g, core, T, topo):
         gather("A", 0, n0 - h0)
         gather("A", n0, L - h1)
         if u == 0:
-            ts(R("TRX", 0, 16), R("TR", 0, 16), 1.0, O.add)
-            ts(R("TRM", 0, 16), R("TR", 0, 16), -16.0, O.mult)
-            convert("S", "SI", 1856, B)
-            convert("S", "SI", 0, 1680)
+            convert("C", "CI", cut[2], cut[3])
         else:
             changes(u - 1)
             if u % 2:
@@ -335,20 +328,26 @@ def rank_program(g, core, T, topo):
             new_counts(u - 1)
             if u == 2:
                 send()
-                new_links(1)
-                update_links(1)
+            if u == 3:
                 store_links("S", B, B + 2 * M)
+                store_counts("S", B + 2 * M, W - M)
         own(0, 0, n0, R("C", x, x + n0))
         if u == 2:
             own(1, 0, LE - n0, R("C", x + n0, x + LE))
             act(R("pC1", LE - n0, n1), R("land", 0, LP), AF.Copy)
         else:
             own(1, 0, n1, R("C", x + n0, x + L))
-        if u % 2:
             mm(R("pY", 0, L), R("IDN", 0, 128), R("S", x, x + L), True, False)
             mm(R("pY", 0, L), R("IDN", 0, 128), R("EA", 0, L), False, True)
             act(R(SV, 0, L), R("pY", 0, L), AF.Identity, 1.0, 1.0)
         gather("V", n0 - h0, n0)
+        if u == 0:
+            ts(R("TRX", 0, 16), R("TR", 0, 16), 1.0, O.add)
+            ts(R("TRM", 0, 16), R("TR", 0, 16), -16.0, O.mult)
+            act(R("S", 1856, B), IND(R("SI", 0, B), R("IDL", 1856 // 16, B // 16)), AF.Copy)
+            act(R("S", 0, 1680), IND(R("SI", 0, B), R("IDL", 0, 1680 // 16)), AF.Copy)
+        if u == 2:
+            link_changes(1)
 
         def keys(b, k):
             nl, l0 = CHUNKS[u][b], b * n0
@@ -375,9 +374,12 @@ def rank_program(g, core, T, topo):
 
         for k in range(16):
             keys(0, k)
+        if u == 2:
+            add_links(1)
         if u % 2:
             lo, hi = ((1680, 1856), (1856, B))[u // 2]
-            update_links(u - 1)
+            link_changes(u - 1)
+            add_links(u - 1)
             store_links("S", lo, hi)
         gather("V", L - h1, L)
         for k in range(16):
@@ -409,7 +411,7 @@ def rank_program(g, core, T, topo):
         same(1)
         ts(R("YG", 0, nt), R("YD", 0, nt), -1.0, O.add, 0.0, O.max)
         act(R("CY", 0, L), IND(win, R("YG", 0, nt)), AF.Copy)
-        act(R("SY", 0, L), IND(R("S", 0, wide), R("YG", 0, nt)), AF.Copy)
+        act(R(SY, 0, L), IND(R("S" if u else "SI", 0, wide), R("YG", 0, nt)), AF.Copy)
         for t in range(2, nt):
             same(t)
         tt(R("DX", 0, nt), R("YD", 0, nt), R("TRX", 0, nt), O.subtract)
@@ -428,8 +430,10 @@ def rank_program(g, core, T, topo):
             lists(2)
             high(2, "EA2")
         if u == 1:
-            total(2, "EA2", "EV2")
-            plus_one(2, "EV2")
+            tt(R("EV2", 0, LANES[2]), R("EA2", 0, LANES[2]), R("S", XCOL[2], XCOL[2] + LANES[2]), O.add)
+            ts(R("SV2", 0, LANES[2]), R("EV2", 0, LANES[2]), 1.0, O.add)
+        if u == 2:
+            new_links(1)
         if u % 2 == 0:
             ent = min(L, LE)
             mm(R("pY", 0, L), R("IDN", 0, 128), R("CY", 0, L), True, False)
@@ -448,19 +452,23 @@ def rank_program(g, core, T, topo):
         tt(R("WY", 0, nt), R("D16", 0, nt), R("S2", 0, nt), O.mult)
         tt(R("WN", 0, nt), R("U16", 0, nt), R("S2", 0, nt), O.mult)
         tt(R("LFY", 0, nt), R("WY", 0, nt), R("TR", 0, nt), O.add)
+        if u % 2:
+            cp(R("LY", 0, nt), R("LFY", 0, nt))
+            cp(IND(R("C", 0, E), R("LY", 0, nt)), R("REST", 0, L))
         tt(R("LFN", 0, nt), R("WN", 0, nt), R("TR", 0, nt), O.add)
-        cp(R("LY", 0, nt), R("LFY", 0, nt))
         ts(R("LN", 0, nt), R("LFN", 0, nt), -float(B + M * u), O.add)
         if u % 2 == 0:
+            cp(R("LY", 0, nt), R("LFY", 0, nt))
             new_links(u)
             lists(u + 1)
-        cp(IND(R("C", 0, E), R("LY", 0, nt)), R("REST", 0, L))
+            cp(IND(R("C", 0, E), R("LY", 0, nt)), R("REST", 0, L))
 
-    store_counts("S", 0, W - M)
+    store_counts("S", 0, B + 2 * M)
     changes(3)
     new_counts(3)
     store_counts("A", W - M, W)
     new_links(3)
-    update_links(3)
+    link_changes(3)
+    add_links(3)
     store_links("S", B + 2 * M, W)
     m["finish"](sent)

from concourse.mybir import AluOpType, ActivationFunctionType

B, LE, LP, M = 2112, 176, 80, 160
W = B + 4 * M
E = W + 256
LANES = (176, 160, 256, 160)
XCOL = (1680, B, 1856, B + 2 * M)
WIDE = (B, B, B, B + 2 * M)
CHUNKS = ((112, 64), (32, 128), (128, 128), (32, 128))
SHARE = ((32, 0), (16, 32), (48, 12), (0, 16))
BEST = ((11, 13), (0, 15), (0, 5), (0, 5))

SCRATCH = {}
PSUM = ("pK0", "pK1", "pC0", "pC1", "pO0", "pO1", "pY", "pW")
for _names, _w, _t in (
        ("CI SI", B, "int32"), ("PI PA", 1, "int32"), ("C S", E, "float32"),
        ("G MN", 4096, "float32"), ("EQ", 4096, "bfloat16"), ("DEAD ONEB", 256, "bfloat16"), ("land", LP, "float32"),
        ("PMX0 PMX1 SEG", 136, "float32"), ("BIAS", 136, "bfloat16"), ("OH0 OH1 IDB BBIG WGT", 128, "bfloat16"),
        ("OS CY SY0 SY1 DD REST TQ EA EA2 THA THB THR SV0 SV1 SV3", 256, "float32"), ("PR YR EV2 SV2", 256, "float16"),
        ("RS", 512, "float16"), ("BB1", 128, "float16"), ("BSEL", 2048, "float16"), ("RSEL", 2048, "bfloat16"),
        ("YO YF YD DX D16 F S2 U16 WN WY LFN LFY QO I16 IDP TR TRX TRM TB", 16, "float32"),
        ("QH QL", 16, "bfloat16"), ("YG LN LY", 16, "uint16"), ("SX0 SX1 SX2 SX3", 256, "uint16"),
        ("T16", B // 16, "float32"), ("IDL", B // 16, "uint16"),
        ("ONEF BH BONES IDN NEG DG SUM", 128, "float32"), ("KEY8", 8, "float32"), ("PF", 1, "float32")):
    for _n in _names.split():
        SCRATCH[_n] = ("sbuf", [128, _w], _t)
for _n in PSUM:
    SCRATCH[_n] = ("psum", [128, 512], "float32")
NDMA = 13
SEMAPHORES = ["qV", "qA", "qP", "qG", "snt", "arr"] + ["d%d" % _i for _i in range(NDMA)]


def R(name, lo, hi, step=1, p=128):
    return (name, lo, hi, step, p)


def IND(win, off):
    return ("@", win, off)


def machine(g, T):
    queue = {"V": g.vector, "A": g.scalar, "P": g.tensor, "G": g, "S": g.sync}
    count = {"V": 0, "A": 0, "P": 0, "G": 0}
    known = {"V": {}, "A": {}, "P": {}, "G": {}, "S": {}}
    clock = {}
    log = {}
    ndma = [0]

    def ap(r):
        if r[0] == "@":
            return ap(r[1]).indirect(ap(r[2]))
        name, lo, hi, step, p = r
        if step == 1:
            return T[name][0:p, lo:hi]
        return T[name][0:p, lo:hi:step]

    def spread(items):
        out = []
        for r in items:
            if not isinstance(r, tuple):
                continue
            if r[0] == "@":
                out.append(r[1])
                out.append(r[2])
            else:
                out.append(r)
        return out

    def needs(q, reads, writes, compute):
        need = {}
        for kind, items in (("r", reads), ("w", writes)):
            for r in items:
                name, lo, hi = r[0], r[1], r[2]
                psum = name in PSUM
                for (l2, h2, k2, ch, val, q2, c2) in log.get(name, []):
                    same = q2 == q and c2 and compute
                    over = lo < h2 and l2 < hi
                    if psum and not same:
                        hit = True
                    elif not over or (kind == "r" and k2 == "r"):
                        hit = False
                    elif same:
                        hit = k2 == "w" and q != "P"
                    else:
                        hit = True
                    if hit:
                        need[ch] = max(need.get(ch, 0), val)
        return need

    def wait(q, need):
        todo = {ch: v for ch, v in need.items() if known[q].get(ch, 0) < v}
        for ch, v in todo.items():
            if not any(c2 != ch and clock[(c2, v2)].get(ch, 0) >= v for c2, v2 in todo.items()):
                queue[q].wait_ge(T.sem[ch], v)
        for ch, v in todo.items():
            for c2, v2 in clock[(ch, v)].items():
                if known[q].get(c2, 0) < v2:
                    known[q][c2] = v2

    def record(q, ch, val, reads, writes, compute):
        snap = dict(known[q])
        if compute:
            for c2, v2 in clock.get((ch, val - 1), {}).items():
                if snap.get(c2, 0) < v2:
                    snap[c2] = v2
        snap[ch] = val
        clock[(ch, val)] = snap
        for kind, items in (("r", reads), ("w", writes)):
            for r in items:
                name, lo, hi, full = r[0], r[1], r[2], r[3] == 1 and r[4] == 128
                old = log.get(name, [])
                if name in PSUM:
                    old = [a for a in old if a[5] == q]
                if kind == "w" and full:
                    old = [a for a in old if not (lo <= a[0] and a[1] <= hi)]
                log[name] = old + [(lo, hi, kind, ch, val, q, compute)]

    def op(q, call, out, reads):
        rd = spread(reads)
        wr = [out]
        if out[0] == "@":
            wr = [(out[1][0], out[1][1], out[1][2], 2, 128)]
            rd.append(out[2])
        wait(q, needs(q, rd, wr, True))
        count[q] += 1
        ch = "q" + q
        call(queue[q]).then_inc(T.sem[ch], 1)
        record(q, ch, count[q], rd, wr, True)

    def dma(q, out, in_, reads, writes):
        wait(q, needs(q, reads, writes, False))
        ch = "d%d" % ndma[0]
        ndma[0] += 1
        queue[q].dma_start(out, in_).then_inc(T.sem[ch], 16)
        record(q, ch, 16, reads, writes, False)

    m = {"ap": ap, "dma": dma}
    m["cp"] = lambda out, a: op("V", lambda e: e.tensor_copy(ap(out), ap(a)), out, [a])
    m["tt"] = lambda out, a, b, o: op("V", lambda e: e.tensor_tensor(ap(out), ap(a), ap(b), o), out, [a, b])

    def ts(out, a, s1, o0, s2=None, o1=None):
        x1 = ap(s1) if isinstance(s1, tuple) else s1
        if o1 is None:
            op("V", lambda e: e.tensor_scalar(ap(out), ap(a), x1, None, o0), out, [a, s1])
        else:
            op("V", lambda e: e.tensor_scalar(ap(out), ap(a), x1, s2, o0, o1), out, [a, s1])
    m["ts"] = ts
    m["fill"] = lambda out, c: op("V", lambda e: e.memset(ap(out), c), out, [])
    m["scan"] = lambda out, a, b, i, o0, o1: op(
        "V", lambda e: e.tensor_tensor_scan(ap(out), ap(a), ap(b), i, o0, o1), out, [a, b])
    m["iota"] = lambda out, pat, base, cm, small: op(
        "G", (lambda e: e.iota(ap(out), pat, base, cm, allow_small_or_imprecise_dtypes=True)) if small else
        (lambda e: e.iota(ap(out), pat, base, cm)), out, [])
    m["keep"] = lambda out, a, pat, cond, base, cm: op(
        "G", lambda e: e.affine_select(ap(out), ap(a), pat, cond, 0.0, base, cm), out, [a])
    m["mm"] = lambda out, l, r, start, stop: op(
        "P", lambda e: e.matmul(ap(out), ap(l), ap(r), start, stop), out, [l, r])

    def act(out, a, func, scale=1.0, bias=0.0):
        x = ap(scale) if isinstance(scale, tuple) else scale
        op("A", lambda e: e.activation(ap(out), ap(a), func, bias=bias, scale=x), out, [a, scale])
    m["act"] = act

    def remote(call, reads, local, n):
        wait("G", needs("G", reads, [], False))
        call()
        record("G", local, n, reads, [], False)
    m["remote"] = remote

    def landed(name, lo, hi, ch, n):
        clock[(ch, n)] = {ch: n}
        log[name] = [(lo, hi, "w", ch, n, "far", False)]
    m["landed"] = landed

    def finish(n):
        need = {"q" + q: count[q] for q in count}
        for i in range(ndma[0]):
            need["d%d" % i] = 16
        need["snt"] = n
        for ch, v in need.items():
            if known["G"].get(ch, 0) < v:
                g.wait_ge(T.sem[ch], v)
    m["finish"] = finish
    return m


def rank_program(g, core, T, topo):
    rank = T.rank_of(core)
    if rank is None:
        return
    O, AF = AluOpType, ActivationFunctionType
    m = machine(g, T)
    cp, tt, ts, fill, scan, mm, act, dma, ap, iota, keep = (
        m["cp"], m["tt"], m["ts"], m["fill"], m["scan"], m["mm"], m["act"], m["dma"], m["ap"], m["iota"], m["keep"])
    n = len(T.cores)
    nxt, prv = T.cores[(rank + 1) % n], T.cores[(rank - 1) % n]
    sent = len(topo.engines(core, nxt))
    m["landed"]("land", 0, LP, "arr", len(topo.engines(prv, core)))

    def load(q, to, src, lo, hi):
        dma(q, T[to][:, lo:hi], T[src][:, lo:hi], [], [R(to, lo, hi)])
    cut = (0, 960, 1680, B)
    load("S", "SI", "s0", 1680, 1856)
    load("A", "CI", "c0", cut[0], cut[1])
    load("S", "CI", "c0", cut[1], cut[2])
    load("A", "CI", "c0", cut[2], cut[3])
    load("S", "SI", "s0", 1856, B)
    load("A", "SI", "s0", 0, 1680)

    fill(R("ONEF", 0, 128), 1.0)
    iota(R("PI", 0, 1), [[0, 1]], 0, 1, False)
    iota(R("T16", 0, B // 16), [[16, B // 16]], 0, 0, True)
    iota(R("I16", 0, 16), [[1, 16]], 0, 0, True)
    keep(R("BH", 0, 128), R("ONEF", 0, 128), [[-16, 8], [0, 16]], O.is_ge, 0, 1)
    keep(R("BONES", 0, 128), R("BH", 0, 128), [[16, 8], [0, 16]], O.is_ge, 15, -1)
    keep(R("IDN", 0, 128), R("ONEF", 0, 128), [[-1, 128]], O.is_equal, 0, 1)
    iota(R("BIAS", 0, 136), [[0, 8], [-1, 17]], 15, 0, True)
    iota(R("ONEB", 0, 256), [[0, 256]], 1, 0, True)
    iota(R("C", B, W), [[0, W - B]], 0, 0, True)
    iota(R("S", B, W), [[0, W - B]], 0, 0, True)
    fill(R("SEG", 0, 136), 1.0)
    fill(R("THA", 0, 256), 0.5)
    fill(R("THB", 0, 256), 0.0)
    fill(R("SEG", 0, 136, 17), 0.0)
    fill(R("THA", 0, 256, 16), 0.0)
    fill(R("THB", 0, 256, 16), 65536.0)
    ts(R("PA", 0, 1), R("PI", 0, 1), 15, O.bitwise_and)
    scan(R("THR", 0, 256), R("THA", 0, 256), R("THB", 0, 256), 0.0, O.mult, O.add)
    cp(R("PF", 0, 1), R("PA", 0, 1))
    ts(R("IDP", 0, 16), R("I16", 0, 16), R("PF", 0, 1), O.is_equal)
    fill(R("BSEL", 0, 2048), 0.0)
    ts(R("TR", 0, 16), R("T16", 0, 16), R("PF", 0, 1), O.add, float(W), O.add)
    ts(R("IDL", 0, B // 16), R("T16", 0, B // 16), R("PF", 0, 1), O.add)
    ts(R("KEY8", 0, 8), R("BONES", 0, 128, 16), 16.0, O.mult)
    cp(R("BB1", 0, 128), R("BONES", 0, 128))
    for i in range(8):
        cp(R("BSEL", 16 * i, 16 * i + 129 * 15 + 1, 129), R("BONES", 16 * i, 16 * i + 16))
    fill(R("BIAS", 16, 136, 17), 1048576.0)
    act(R("IDB", 0, 128), R("IDN", 0, 128), AF.Copy)
    act(R("BBIG", 0, 128), R("BONES", 0, 128), AF.Copy, 65536.0)
    act(R("NEG", 0, 128), R("IDN", 0, 128), AF.Copy, -1.0)
    for i in range(16):
        act(R("RSEL", 128 * i, 128 * i + 128), R("BONES", 0, 128), AF.Copy, R("IDP", i, i + 1))
    tt(R("DG", 0, 128), R("IDN", 0, 128), R("THR", 0, 128), O.mult)
    scan(R("SUM", 0, 128), R("ONEF", 0, 128), R("DG", 0, 128), 0.0, O.mult, O.add)
    ts(R("WGT", 0, 128), R("BONES", 0, 128), R("SUM", 127, 128), O.mult, 0.5, O.mult)

    def high(u, to):
        ts(R(to, 0, LANES[u]), R("S", XCOL[u], XCOL[u] + LANES[u]), 2047.5, O.is_gt, -4096.0, O.mult)

    def lists(u):
        cp(R("SX%d" % u, 0, LANES[u]), R("S", XCOL[u], XCOL[u] + LANES[u]))

    def convert(to, src, lo, hi):
        cp(R(to, lo, hi), R(src, lo, hi))

    convert("S", "SI", 1680, 1856)
    lists(0)
    high(0, "EA")
    convert("C", "CI", cut[0], cut[1])
    convert("C", "CI", cut[1], cut[2])

    def new_counts(u):
        tt(IND(R("C", B + M * u, E), R("LN", 0, LANES[u] // 16)), R("CY", 0, LANES[u]), R("REST", 0, LANES[u]), O.subtract)

    def new_links(u):
        cp(IND(R("S", B + M * u, E), R("LN", 0, LANES[u] // 16)), R("SY%d" % (u % 2), 0, LANES[u]))

    def changes(u):
        nt = LANES[u] // 16
        tt(R("QO", 0, nt), R("LFN", 0, nt), R("LFY", 0, nt), O.subtract)
        cp(R("QH", 0, nt), R("QO", 0, nt))
        tt(R("QL", 0, nt), R("QO", 0, nt), R("QH", 0, nt), O.subtract)
        for i in range(16):
            mm(R("pW", i, LANES[u], 16), R("RSEL", 128 * i, 128 * i + 128), R("QH", 0, nt), True, False)
            mm(R("pW", i, LANES[u], 16), R("RSEL", 128 * i, 128 * i + 128), R("QL", 0, nt), False, True)

    def link_changes(u):
        tt(R("TQ", 0, LANES[u]), R("OS", 0, LANES[u]), R("pW", 0, LANES[u]), O.mult)

    def add_links(u):
        L, x = LANES[u], XCOL[u]
        if u == 3:
            tt(R("S", x, x + L), R("S", x, x + L), R("TQ", 0, L), O.add)
        else:
            mm(R("pW", 0, L), R("IDN", 0, 128), R("S", x, x + L), True, False)
            mm(R("pW", 0, L), R("IDN", 0, 128), R("TQ", 0, L), False, True)
            act(R("S", x, x + L), R("pW", 0, L), AF.Copy)

    def send():
        rid, pid = topo.addr(nxt)[:2]
        src = B + M
        m["remote"](lambda: g.remote_dma(out_ap=T.land[:], in_ap=T.C[:, src:src + LP], remote_sem=T.sem.arr,
                                         local_sem=T.sem.snt, pid=pid, routing_id=rid, dma_engine_mask=topo.mask(core, nxt)),
                    [R("C", src, src + LP)], "snt", sent)

    def store_links(q, lo, hi):
        dma(q, T.ys[:, lo - 1680:hi - 1680], T.S[:, lo:hi], [R("S", lo, hi)], [])

    def store_counts(q, lo, hi):
        dma(q, T.yc[:, lo:hi], T.C[:, lo:hi], [R("C", lo, hi)], [])

    for u in range(4):
        L, x, wide = LANES[u], XCOL[u], WIDE[u]
        nt = L // 16
        n0, n1 = CHUNKS[u]
        h0, h1 = SHARE[u]
        win = R("C" if u else "CI", 0, wide)
        SX, SV, SY = "SX%d" % u, "SV%d" % u, "SY%d" % (u % 2)

        def gather(q, lo, hi):
            if lo < hi and q == "A":
                act(R("G", 16 * lo, 16 * hi), IND(win, R(SX, lo, hi)), AF.Copy)
            elif lo < hi:
                cp(R("G", 16 * lo, 16 * hi), IND(win, R(SX, lo, hi)))

        def own(b, lo, hi, src):
            mm(R("pC%d" % b, lo, hi), R("IDN", 0, 128), src, True, True)

        gather("A", 0, n0 - h0)
        gather("A", n0, L - h1)
        if u == 0:
            convert("C", "CI", cut[2], cut[3])
        else:
            changes(u - 1)
            if u % 2:
                high(u, "EA")
            new_counts(u - 1)
            if u == 2:
                send()
            if u == 3:
                store_links("S", B, B + 2 * M)
                store_counts("S", B + 2 * M, W - M)
        own(0, 0, n0, R("C", x, x + n0))
        if u == 2:
            own(1, 0, LE - n0, R("C", x + n0, x + LE))
            act(R("pC1", LE - n0, n1), R("land", 0, LP), AF.Copy)
        else:
            own(1, 0, n1, R("C", x + n0, x + L))
            mm(R("pY", 0, L), R("IDN", 0, 128), R("S", x, x + L), True, False)
            mm(R("pY", 0, L), R("IDN", 0, 128), R("EA", 0, L), False, True)
            act(R(SV, 0, L), R("pY", 0, L), AF.Identity, 1.0, 1.0)
        gather("V", n0 - h0, n0)
        if u == 0:
            ts(R("TRX", 0, 16), R("TR", 0, 16), 1.0, O.add)
            ts(R("TRM", 0, 16), R("TR", 0, 16), -16.0, O.mult)
            act(R("S", 1856, B), IND(R("SI", 0, B), R("IDL", 1856 // 16, B // 16)), AF.Copy)
            act(R("S", 0, 1680), IND(R("SI", 0, B), R("IDL", 0, 1680 // 16)), AF.Copy)
        if u == 2:
            link_changes(1)

        def keys(b, k):
            nl, l0 = CHUNKS[u][b], b * n0
            tt(R("MN", 16 * l0 + k * nl, 16 * l0 + (k + 1) * nl), R("G", 16 * l0 + k, 16 * (l0 + nl), 16),
               R("pC%d" % b, 0, nl), O.min)
            if k == 0:
                mm(R("pK%d" % b, 0, 136, 1, nl), R("ONEB", 0, nl, 1, 1), R("BIAS", 0, 136, 1, 1), True, False)
            mm(R("pK%d" % b, k, 136, 17, nl), R("MN", 16 * l0 + k * nl, 16 * l0 + (k + 1) * nl), R("KEY8", 0, 8),
               False, k == 15)

        def best(b):
            nl = CHUNKS[u][b]
            K, X = "pK%d" % b, "PMX%d" % b
            scan(R(X, 0, 136, 1, nl), R("SEG", 0, 136, 1, nl), R(K, 0, 136, 1, nl), 0.0, O.mult, O.max)
            for j in range(8):
                ts(R("OH%d" % b, 16 * j, 16 * j + 16, 1, nl), R(K, 17 * j, 17 * j + 16, 1, nl),
                   R(X, 17 * j + 16, 17 * j + 17, 1, nl), O.is_equal)
            mm(R("pO%d" % b, 0, nl), R("OH%d" % b, 0, 128, 1, nl), R("IDB", 0, nl, 1, nl), True, True)

        def pick(b):
            nl, l0 = CHUNKS[u][b], b * n0
            tt(R("PR", l0, l0 + nl), R("pO%d" % b, 0, nl), R(SV, l0, l0 + nl), O.mult)
            act(R("OS", l0, l0 + nl), R("pO%d" % b, 0, nl), AF.Copy)

        for k in range(16):
            keys(0, k)
        if u == 2:
            add_links(1)
        if u % 2:
            lo, hi = ((1680, 1856), (1856, B))[u // 2]
            link_changes(u - 1)
            add_links(u - 1)
            store_links("S", lo, hi)
        gather("V", L - h1, L)
        for k in range(16):
            if k == BEST[u][0]:
                best(0)
            keys(1, k)
            if k == BEST[u][1]:
                pick(0)
        ts(R("TB", 0, 16), R("TRM", 0, 16), 16.0 * (B + M * u - 1), O.add)
        best(1)
        pick(1)
        mm(R("pY", 0, L), R("BB1", 0, 128), R("PR", 0, L), True, True)
        for i in range(16):
            mm(R("pK0", 256, 256 + nt), R("BSEL", 128 * i, 128 * i + 128), R("PR", i, L, 16), i == 0, i == 15)
        cp(R("YR", 0, L), R("pY", 0, L))
        ts(R("DEAD", 0, L), R("YR", 0, L), 0.0, O.is_equal)
        mm(R("pW", 0, L), R("BBIG", 0, 128), R("DEAD", 0, L), True, False)
        cp(R("YO", 0, nt), R("pK0", 256, 256 + nt))
        ts(R("YF", 0, nt), R("YO", 0, nt), 0.0, O.is_lt, 4096.0, O.mult)

        def same(t):
            o = 256 * t
            ts(R("EQ", o + 16 * t, o + L), R("YR", 16 * t, L), R("YO", t, t + 1), O.is_equal)
            mm(R("pW", 16 * t, 16 * t + 16), R("WGT", 0, 128), R("EQ", o + 16 * t, o + 16 * t + 16), False, t == nt - 1)
            if t < nt - 1:
                mm(R("pW", 16 * t + 16, L), R("BBIG", 0, 128), R("EQ", o + 16 * t + 16, o + L), False, False)
        same(0)
        tt(R("YD", 0, nt), R("YF", 0, nt), R("YO", 0, nt), O.add)
        same(1)
        ts(R("YG", 0, nt), R("YD", 0, nt), -1.0, O.add, 0.0, O.max)
        act(R("CY", 0, L), IND(win, R("YG", 0, nt)), AF.Copy)
        act(R(SY, 0, L), IND(R("S" if u else "SI", 0, wide), R("YG", 0, nt)), AF.Copy)
        for t in range(2, nt):
            same(t)
        tt(R("DX", 0, nt), R("YD", 0, nt), R("TRX", 0, nt), O.subtract)
        if u % 2:
            l0 = 0
            for b, nl in enumerate(CHUNKS[u]):
                tt(R("DD", l0, l0 + nl), R("CY", l0, l0 + nl), R("pC%d" % b, 0, nl), O.subtract)
                l0 += nl
            act(R("REST", 0, L), R("DD", 0, L), AF.Relu)
        ts(R("D16", 0, nt), R("DX", 0, nt), 16.0, O.mult)
        tt(R("RS", L, 2 * L), R("pW", 0, L), R("THR", 0, L), O.is_lt)
        scan(R("RS", 0, L), R("ONEB", 0, L), R("RS", L, 2 * L), 0.0, O.mult, O.add)
        for i in range(16):
            mm(R("pK1", 256, 256 + 2 * nt), R("BSEL", 128 * i, 128 * i + 128), R("RS", i, 2 * L, 16), i == 0, i == 15)
        if u == 0:
            lists(2)
            high(2, "EA2")
        if u == 1:
            tt(R("EV2", 0, LANES[2]), R("EA2", 0, LANES[2]), R("S", XCOL[2], XCOL[2] + LANES[2]), O.add)
            ts(R("SV2", 0, LANES[2]), R("EV2", 0, LANES[2]), 1.0, O.add)
        if u == 2:
            new_links(1)
        if u % 2 == 0:
            ent = min(L, LE)
            mm(R("pY", 0, L), R("IDN", 0, 128), R("CY", 0, L), True, False)
            mm(R("pY", 0, ent), R("NEG", 0, 128), R("C", x, x + ent), False, ent == L)
            if ent < L:
                mm(R("pY", ent, L), R("NEG", 0, 128), R("land", 0, LP), False, True)
            act(R("REST", 0, L), R("pY", 0, L), AF.Relu)

        if L > M:
            ts(R("F", 0, nt), R("pK1", 256, 256 + nt), 16.0 * M + 0.5, O.is_le, 1.0 / 256, O.mult)
            tt(R("U16", 0, nt), R("pK1", 256, 256 + nt), R("TB", 0, nt), O.add)
            tt(R("S2", 0, nt), R("F", 0, nt), R("pK1", 256 + nt, 256 + 2 * nt), O.mult)
        else:
            ts(R("S2", 0, nt), R("pK1", 256 + nt, 256 + 2 * nt), 1.0 / 256, O.mult)
            tt(R("U16", 0, nt), R("pK1", 256, 256 + nt), R("TB", 0, nt), O.add)
        tt(R("WY", 0, nt), R("D16", 0, nt), R("S2", 0, nt), O.mult)
        tt(R("WN", 0, nt), R("U16", 0, nt), R("S2", 0, nt), O.mult)
        tt(R("LFY", 0, nt), R("WY", 0, nt), R("TR", 0, nt), O.add)
        if u % 2:
            cp(R("LY", 0, nt), R("LFY", 0, nt))
            cp(IND(R("C", 0, E), R("LY", 0, nt)), R("REST", 0, L))
        tt(R("LFN", 0, nt), R("WN", 0, nt), R("TR", 0, nt), O.add)
        ts(R("LN", 0, nt), R("LFN", 0, nt), -float(B + M * u), O.add)
        if u % 2 == 0:
            cp(R("LY", 0, nt), R("LFY", 0, nt))
            new_links(u)
            lists(u + 1)
            cp(IND(R("C", 0, E), R("LY", 0, nt)), R("REST", 0, L))

    store_counts("S", 0, B + 2 * M)
    changes(3)
    new_counts(3)
    store_counts("A", W - M, W)
    new_links(3)
    link_changes(3)
    add_links(3)
    store_links("S", B + 2 * M, W)
    m["finish"](sent)
